import numpy as np
import ml_dtypes


def mxq(x, axis, fmt="e4m3"):
    dtype, down = {"e4m3": (ml_dtypes.float8_e4m3fn, 7), "e5m2": (ml_dtypes.float8_e5m2, 14)}[fmt]
    v = np.moveaxis(np.asarray(x, np.float32).astype(ml_dtypes.bfloat16).astype(np.float64), axis, -1)
    blocks = v.reshape(v.shape[:-1] + (-1, 32))
    amax = np.abs(blocks).max(-1, keepdims=True)
    byte = np.maximum(np.where(amax > 0, np.frexp(amax)[1] - 1 + 127, 0) - down, 1)
    scale = np.exp2(byte - 127.0)
    codes = (blocks / scale).astype(np.float32).astype(dtype).astype(np.float64)
    return np.moveaxis((codes * scale).reshape(v.shape), -1, axis)


WIDE = False


def mx_kscale(k):
    if not WIDE:
        return np.ones(k)
    levels = np.array([10, -10, 5, -5, 0])
    if k % 512:
        return np.exp2(np.random.permutation(np.resize(levels, k // 32))).repeat(32)
    a = np.empty((k // 512, 16))
    for p in range(k // 512):
        a[p, :8] = np.random.permutation(np.resize(levels, 8))
        for g in range(8):
            far = levels[np.abs(levels - a[p, g]) >= 10]
            a[p, g + 8] = far[np.random.randint(len(far))]
    return np.exp2(a.ravel()).repeat(32)


def f64(x):
    return np.asarray(x).astype(np.float64)


def striped(idx):
    return np.tile(idx.reshape(-1, 16).T, (8, 1)).astype(np.uint16)


def unstriped(offs):
    return offs[:16].T.reshape(-1).astype(np.int64)


def relu(v):
    return np.maximum(v, 0.0)


K, T, D, S, V, N = 1024, 2048, 4, 512, 128, 512


def setup_inputs():
    n = np.random.standard_normal
    s = mx_kscale(K)[:, None]
    return {
        "xT": (n((K, T)) * s).astype(np.float32),
        "w": (n((D, K, N)) / np.sqrt(D * K) / s[None]).astype(np.float32),
        "b": (0.3 * n((N, 1))).astype(np.float32),
        "offs": striped(np.random.permutation(T)[:S]),
    }


def reference(xT, w, b, offs):
    idx = unstriped(offs)
    xq = mxq(f64(xT)[:, idx], 0, "e4m3")
    wq = mxq(f64(w), 1, "e4m3")
    y = sum(wq[d].T @ xq[:, d * V:(d + 1) * V] for d in range(D))
    y = relu(y + f64(b))
    return y

@@ -1,0 +1,168 @@
+from contextlib import ExitStack
+
+import concourse.mybir as mybir
+from concourse.masks import make_identity
+
+K, T, D, S, V, N = 1024, 2048, 4, 512, 128, 512
+FLOPS = 2 * K * N * S
+
+F32 = mybir.dt.float32
+BF16 = mybir.dt.bfloat16
+U32 = mybir.dt.uint32
+U16 = mybir.dt.uint16
+U8 = mybir.dt.uint8
+FP8X4 = mybir.dt.float8_e4m3fn_x4
+RELU = mybir.ActivationFunctionType.Relu
+
+P = 128
+PACK = 4
+K_PASS = P * PACK
+PASSES = K // K_PASS
+M_TILES = N // P
+
+LAST = (3, 1)
+
+
+def tile_picked_merge_lin_relu_sub_e_kernel(tc, xT, w, b, offs, out):
+    nc = tc.nc
+    x_rows = xT.rearrange("(a p j) t -> a j p t", a=PASSES, j=PACK)
+    w_rows = w.rearrange("d (a p j) m -> d a p j m", a=PASSES, j=PACK)
+
+    with ExitStack() as ctx:
+        held = ctx.enter_context(tc.tile_pool(name="held", bufs=1))
+        ring = ctx.enter_context(tc.tile_pool(name="ring", bufs=4))
+        psum = ctx.enter_context(tc.psum_pool(name="psum", bufs=1))
+
+        offsets = held.tile([P, S // 16], U16, name="offsets")
+        bias_rows = held.tile([P, P], F32, name="bias_rows")
+        bias = held.tile([P, M_TILES], F32, name="bias")
+        ident = held.tile([P, P], F32, name="ident")
+
+        planes = {}
+        raws = {}
+
+        def load_plane(a, j):
+            planes[a, j] = held.tile([P, T], F32, name=f"plane{a}{j}")
+            nc.sync.dma_start(planes[a, j][:], x_rows[a, j])
+
+        def load_w(d, a, c0, c1):
+            raws[d, a, c0] = held.tile([P, PACK, c1 - c0], F32, name=f"raw{d}{a}{c0}")
+            nc.sync.dma_start(raws[d, a, c0][:], w_rows[d, a, :, :, c0:c1])
+
+        picked = [held.tile([P, PACK, S], F32, name=f"picked{a}") for a in range(PASSES)]
+        x_codes = [held.tile([P, S], U32, align_bytes=64, name=f"x_codes{a}") for a in range(PASSES)]
+        x_scales = [held.tile([P, S], U8, align_bytes=64, name=f"x_scales{a}") for a in range(PASSES)]
+        acc = [psum.tile([P, V], F32, name=f"acc{t}") for t in range(M_TILES)]
+
+        def interleave(dst, src, c0, c1, engine_copy):
+            engine_copy(
+                dst[:, c0:c1, :].rearrange("p (c i) j -> p c j i", i=4),
+                src[:, :, c0:c1].rearrange("p j (c i) -> p c j i", i=4),
+            )
+
+        def gather(a, j):
+            nc.vector.tensor_copy(picked[a][:, j, :], planes[a, j][:].indirect(offsets[:]))
+
+        groupeds = {}
+
+        def spread_x(a):
+            grouped = ring.tile([P, S, PACK], BF16, align_bytes=64, name="x_grouped")
+            groupeds["x", a] = grouped
+            interleave(grouped, picked[a], 0, S, nc.scalar.copy)
+
+        def quantise_x(a):
+            nc.vector.quantize_mx(
+                out=x_codes[a][:].bitcast(FP8X4),
+                scales=x_scales[a][:],
+                in_=groupeds["x", a][:].rearrange("p c j -> p (c j)"),
+            )
+
+        def spread_w(d, a, c0, c1):
+            width = c1 - c0
+            grouped = ring.tile([P, width, PACK], BF16, align_bytes=64, name=f"w_grouped{width}")
+            groupeds[d, a, c0] = grouped
+            half = width // 2
+            interleave(grouped, raws[d, a, c0], 0, half, nc.vector.tensor_copy)
+            interleave(grouped, raws[d, a, c0], half, width, nc.scalar.copy)
+
+        order = [(0, 0), (1, 0), (0, 1), (1, 1), (2, 0), (2, 1), (3, 0), (3, 1)]
+
+        def multiply_w(d, a, c0, c1):
+            width = c1 - c0
+            codes = held.tile([P, width], U32, align_bytes=64, name=f"w_codes{d}{a}{c0}")
+            scales = held.tile([P, width], U8, align_bytes=64, name=f"w_scales{d}{a}{c0}")
+            nc.vector.quantize_mx(
+                out=codes[:].bitcast(FP8X4),
+                scales=scales[:],
+                in_=groupeds[d, a, c0][:].rearrange("p c j -> p (c j)"),
+            )
+            for m0 in range(c0, c1, P):
+                cols = slice(m0 - c0, m0 - c0 + P)
+                tokens = slice(d * V, (d + 1) * V)
+                nc.tensor.matmul_mx(
+                    out=acc[m0 // P][:],
+                    lhsT=codes[:, cols].bitcast(FP8X4),
+                    lhsT_scale=scales[:, cols],
+                    rhs=x_codes[a][:, tokens].bitcast(FP8X4),
+                    rhs_scale=x_scales[a][:, tokens],
+                    start=((d, a) == order[0]),
+                    stop=((d, a) == order[-1]),
+                )
+
+        def finish(t):
+            result = held.tile([P, V], F32, name=f"result{t}")
+            nc.scalar.activation(result[:], acc[t][:], RELU, bias=bias[:, t : t + 1])
+            nc.sync.dma_start(out[t * P : (t + 1) * P, :], result[:])
+
+        nc.gpsimd.memset(bias_rows[:], 0.0)
+        nc.scalar.dma_start(bias_rows[0:M_TILES, :], b.rearrange("(t p) o -> t (p o)", p=P))
+        make_identity(nc, ident[:])
+        turned = psum.tile([P, P], F32, name="turned")
+        nc.tensor.transpose(turned[:], bias_rows[:], ident[:])
+        nc.vector.tensor_copy(bias[:], turned[:, 0:M_TILES])
+
+        pieces = [(3, 1, 0, 256), (3, 1, 256, 384), (3, 1, 384, 512)]
+        loads = [
+            ("x", 0, 0), ("x", 0, 1), ("w", 0, 0, 0, N), ("x", 0, 2), ("x", 0, 3), ("w", 1, 0, 0, N),
+            ("x", 1, 0), ("x", 1, 1), ("w", 0, 1, 0, N), ("x", 1, 2), ("x", 1, 3), ("w", 1, 1, 0, N),
+            ("w", 2, 0, 0, N), ("w", 2, 1, 0, N), ("w", 3, 0, 0, N),
+        ] + [("w",) + piece for piece in pieces]
+        for i, load in enumerate(loads):
+            if load[0] == "x":
+                load_plane(*load[1:])
+            else:
+                load_w(*load[1:])
+            if i == 0:
+                nc.sync.dma_start(offsets[:], offs)
+
+        pending = []
+        ready_x = set()
+        for load in loads:
+            if load[0] == "x":
+                gather(*load[1:])
+                a = load[1]
+                if load[2] == PACK - 1:
+                    spread_x(a)
+                    todo = ("x", a)
+                else:
+                    todo = None
+            else:
+                spread_w(*load[1:])
+                todo = load
+            keep = []
+            for item in pending:
+                if item[0] == "x":
+                    quantise_x(item[1])
+                    ready_x.add(item[1])
+                elif item[2] in ready_x:
+                    multiply_w(*item[1:])
+                    if item[1:3] == LAST:
+                        for t in range(item[3] // P, item[4] // P):
+                            finish(t)
+                else:
+                    keep.append(item)
+            pending = keep + ([todo] if todo else [])
+        for item in pending:
+            multiply_w(*item[1:])
+            for t in range(item[3] // P, item[4] // P):
+                finish(t)

@@ -13,6 +13,7 @@ U16 = mybir.dt.uint16
 U8 = mybir.dt.uint8
 FP8X4 = mybir.dt.float8_e4m3fn_x4
 RELU = mybir.ActivationFunctionType.Relu
+ADD, MAX = mybir.AluOpType.add, mybir.AluOpType.max
 
 P = 128
 PACK = 4
@@ -20,12 +21,10 @@ K_PASS = P * PACK
 PASSES = K // K_PASS
 M_TILES = N // P
 
-LAST = (3, 1)
-
 
 def tile_picked_merge_lin_relu_sub_e_kernel(tc, xT, w, b, offs, out):
     nc = tc.nc
-    x_rows = xT.rearrange("(a p j) t -> a j p t", a=PASSES, j=PACK)
+    x_rows = xT.rearrange("(a p j) t -> a p j t", a=PASSES, j=PACK)
     w_rows = w.rearrange("d (a p j) m -> d a p j m", a=PASSES, j=PACK)
 
     with ExitStack() as ctx:
@@ -37,22 +36,20 @@ def tile_picked_merge_lin_relu_sub_e_kernel(tc, xT, w, b, offs, out):
         bias_rows = held.tile([P, P], F32, name="bias_rows")
         bias = held.tile([P, M_TILES], F32, name="bias")
         ident = held.tile([P, P], F32, name="ident")
-
-        planes = {}
-        raws = {}
-
-        def load_plane(a, j):
-            planes[a, j] = held.tile([P, T], F32, name=f"plane{a}{j}")
-            nc.sync.dma_start(planes[a, j][:], x_rows[a, j])
-
-        def load_w(d, a, c0, c1):
-            raws[d, a, c0] = held.tile([P, PACK, c1 - c0], F32, name=f"raw{d}{a}{c0}")
-            nc.sync.dma_start(raws[d, a, c0][:], w_rows[d, a, :, :, c0:c1])
-
+        planes, raws, groupeds, codes, scales = {}, {}, {}, {}, {}
         picked = [held.tile([P, PACK, S], F32, name=f"picked{a}") for a in range(PASSES)]
         x_codes = [held.tile([P, S], U32, align_bytes=64, name=f"x_codes{a}") for a in range(PASSES)]
         x_scales = [held.tile([P, S], U8, align_bytes=64, name=f"x_scales{a}") for a in range(PASSES)]
         acc = [psum.tile([P, V], F32, name=f"acc{t}") for t in range(M_TILES)]
+        results = [held.tile([P, V], F32, name=f"result{t}") for t in range(M_TILES)]
+
+        def load_x(a, j0):
+            planes[a, j0] = held.tile([P, 2, T], F32, name=f"planes{a}{j0}")
+            nc.sync.dma_start(planes[a, j0][:], x_rows[a, :, j0 : j0 + 2, :])
+
+        def load_w(d, a, c0, c1):
+            raws[d, a, c0] = held.tile([P, PACK, c1 - c0], F32, name=f"raw{d}{a}{c0}")
+            nc.sync.dma_start(raws[d, a, c0][:], w_rows[d, a, :, :, c0:c1])
 
         def interleave(dst, src, c0, c1, engine_copy):
             engine_copy(
@@ -60,109 +57,102 @@ def tile_picked_merge_lin_relu_sub_e_kernel(tc, xT, w, b, offs, out):
                 src[:, :, c0:c1].rearrange("p j (c i) -> p c j i", i=4),
             )
 
-        def gather(a, j):
-            nc.vector.tensor_copy(picked[a][:, j, :], planes[a, j][:].indirect(offsets[:]))
+        def gather(a, j0):
+            for u in range(2):
+                nc.vector.tensor_copy(picked[a][:, j0 + u, :], planes[a, j0][:, u, :].indirect(offsets[:]))
 
-        groupeds = {}
-
-        def spread_x(a):
-            grouped = ring.tile([P, S, PACK], BF16, align_bytes=64, name="x_grouped")
-            groupeds["x", a] = grouped
-            interleave(grouped, picked[a], 0, S, nc.scalar.copy)
+        def spread_x(a, c0, c1):
+            if c0 == 0:
+                groupeds[a] = ring.tile([P, S, PACK], BF16, align_bytes=64, name="x_grouped")
+            interleave(groupeds[a], picked[a], c0, c1, nc.scalar.copy)
 
         def quantise_x(a):
             nc.vector.quantize_mx(
                 out=x_codes[a][:].bitcast(FP8X4),
                 scales=x_scales[a][:],
-                in_=groupeds["x", a][:].rearrange("p c j -> p (c j)"),
+                in_=groupeds[a][:].rearrange("p c j -> p (c j)"),
             )
 
-        def spread_w(d, a, c0, c1):
+        def spread_w(d, a, c0, c1, v_cols):
             width = c1 - c0
             grouped = ring.tile([P, width, PACK], BF16, align_bytes=64, name=f"w_grouped{width}")
             groupeds[d, a, c0] = grouped
-            half = width // 2
-            interleave(grouped, raws[d, a, c0], 0, half, nc.vector.tensor_copy)
-            interleave(grouped, raws[d, a, c0], half, width, nc.scalar.copy)
+            interleave(grouped, raws[d, a, c0], 0, v_cols, nc.vector.tensor_copy)
+            interleave(grouped, raws[d, a, c0], v_cols, width, nc.scalar.copy)
 
-        order = [(0, 0), (1, 0), (0, 1), (1, 1), (2, 0), (2, 1), (3, 0), (3, 1)]
-
-        def multiply_w(d, a, c0, c1):
-            width = c1 - c0
-            codes = held.tile([P, width], U32, align_bytes=64, name=f"w_codes{d}{a}{c0}")
-            scales = held.tile([P, width], U8, align_bytes=64, name=f"w_scales{d}{a}{c0}")
+        def quantise_w(d, a, c0, c1):
+            codes[d, a, c0] = held.tile([P, c1 - c0], U32, align_bytes=64, name=f"w_codes{d}{a}{c0}")
+            scales[d, a, c0] = held.tile([P, c1 - c0], U8, align_bytes=64, name=f"w_scales{d}{a}{c0}")
             nc.vector.quantize_mx(
-                out=codes[:].bitcast(FP8X4),
-                scales=scales[:],
+                out=codes[d, a, c0][:].bitcast(FP8X4),
+                scales=scales[d, a, c0][:],
                 in_=groupeds[d, a, c0][:].rearrange("p c j -> p (c j)"),
             )
+
+        def multiply(d, a, c0, c1, first=False, last=False):
+            tokens = slice(d * V, (d + 1) * V)
             for m0 in range(c0, c1, P):
                 cols = slice(m0 - c0, m0 - c0 + P)
-                tokens = slice(d * V, (d + 1) * V)
                 nc.tensor.matmul_mx(
                     out=acc[m0 // P][:],
-                    lhsT=codes[:, cols].bitcast(FP8X4),
-                    lhsT_scale=scales[:, cols],
+                    lhsT=codes[d, a, c0][:, cols].bitcast(FP8X4),
+                    lhsT_scale=scales[d, a, c0][:, cols],
                     rhs=x_codes[a][:, tokens].bitcast(FP8X4),
                     rhs_scale=x_scales[a][:, tokens],
-                    start=((d, a) == order[0]),
-                    stop=((d, a) == order[-1]),
+                    start=first,
+                    stop=last,
                 )
 
-        def finish(t):
-            result = held.tile([P, V], F32, name=f"result{t}")
-            nc.scalar.activation(result[:], acc[t][:], RELU, bias=bias[:, t : t + 1])
-            nc.sync.dma_start(out[t * P : (t + 1) * P, :], result[:])
+        def finish(t, on_vector=False):
+            if on_vector:
+                nc.vector.tensor_scalar(results[t][:], acc[t][:], bias[:, t : t + 1], 0.0, op0=ADD, op1=MAX)
+            else:
+                nc.scalar.activation(results[t][:], acc[t][:], RELU, bias=bias[:, t : t + 1])
+            nc.sync.dma_start(out[t * P : (t + 1) * P, :], results[t][:])
 
         nc.gpsimd.memset(bias_rows[:], 0.0)
-        nc.scalar.dma_start(bias_rows[0:M_TILES, :], b.rearrange("(t p) o -> t (p o)", p=P))
         make_identity(nc, ident[:])
         turned = psum.tile([P, P], F32, name="turned")
-        nc.tensor.transpose(turned[:], bias_rows[:], ident[:])
-        nc.vector.tensor_copy(bias[:], turned[:, 0:M_TILES])
 
-        pieces = [(3, 1, 0, 256), (3, 1, 256, 384), (3, 1, 384, 512)]
-        loads = [
-            ("x", 0, 0), ("x", 0, 1), ("w", 0, 0, 0, N), ("x", 0, 2), ("x", 0, 3), ("w", 1, 0, 0, N),
-            ("x", 1, 0), ("x", 1, 1), ("w", 0, 1, 0, N), ("x", 1, 2), ("x", 1, 3), ("w", 1, 1, 0, N),
-            ("w", 2, 0, 0, N), ("w", 2, 1, 0, N), ("w", 3, 0, 0, N),
-        ] + [("w",) + piece for piece in pieces]
-        for i, load in enumerate(loads):
-            if load[0] == "x":
-                load_plane(*load[1:])
-            else:
-                load_w(*load[1:])
-            if i == 0:
-                nc.sync.dma_start(offsets[:], offs)
+        def turn_bias():
+            nc.tensor.transpose(turned[:], bias_rows[:], ident[:])
+            nc.vector.tensor_copy(bias[:], turned[:, 0:M_TILES])
 
-        pending = []
-        ready_x = set()
-        for load in loads:
-            if load[0] == "x":
-                gather(*load[1:])
-                a = load[1]
-                if load[2] == PACK - 1:
-                    spread_x(a)
-                    todo = ("x", a)
-                else:
-                    todo = None
-            else:
-                spread_w(*load[1:])
-                todo = load
-            keep = []
-            for item in pending:
-                if item[0] == "x":
-                    quantise_x(item[1])
-                    ready_x.add(item[1])
-                elif item[2] in ready_x:
-                    multiply_w(*item[1:])
-                    if item[1:3] == LAST:
-                        for t in range(item[3] // P, item[4] // P):
-                            finish(t)
-                else:
-                    keep.append(item)
-            pending = keep + ([todo] if todo else [])
-        for item in pending:
-            multiply_w(*item[1:])
-            for t in range(item[3] // P, item[4] // P):
-                finish(t)
+        load_x(0, 0)
+        nc.sync.dma_start(offsets[:], offs)
+        load_x(0, 2)
+        nc.sync.dma_start(bias_rows[0:M_TILES, :], b.rearrange("(t p) o -> t (p o)", p=P))
+        load_x(1, 0)
+        load_x(1, 2)
+        chunks = [(d, a, 0, N) for a in range(PASSES) for d in range(D)][:-1]
+        chunks += [(3, 1, 0, 256), (3, 1, 256, 384), (3, 1, 384, 512)]
+        for chunk in chunks:
+            load_w(*chunk)
+
+        gather(0, 0)
+        gather(0, 2)
+        spread_x(0, 0, S)
+        gather(1, 0)
+        quantise_x(0)
+        turn_bias()
+        gather(1, 2)
+        spread_w(*chunks[0], 224)
+        spread_x(1, 0, 256)
+        spread_w(*chunks[1], 224)
+        quantise_w(*chunks[0])
+        multiply(*chunks[0], first=True)
+        spread_x(1, 256, S)
+        spread_w(*chunks[2], 224)
+        quantise_w(*chunks[1])
+        multiply(*chunks[1])
+        quantise_x(1)
+        for before, now in zip(chunks[2:], chunks[3:]):
+            spread_w(*now, 224 if now[3] - now[2] == N else (now[3] - now[2]) // 2)
+            quantise_w(*before)
+            multiply(*before, last=before[:2] == (3, 1))
+        quantise_w(*chunks[-1])
+        multiply(*chunks[-1], last=True)
+        finish(0)
+        finish(1)
+        finish(2)
+        finish(3, on_vector=True)

from contextlib import ExitStack

import concourse.mybir as mybir
from concourse.masks import make_identity

K, T, D, S, V, N = 1024, 2048, 4, 512, 128, 512
FLOPS = 2 * K * N * S

F32 = mybir.dt.float32
BF16 = mybir.dt.bfloat16
U32 = mybir.dt.uint32
U16 = mybir.dt.uint16
U8 = mybir.dt.uint8
FP8X4 = mybir.dt.float8_e4m3fn_x4
RELU = mybir.ActivationFunctionType.Relu
ADD, MAX = mybir.AluOpType.add, mybir.AluOpType.max

P = 128
PACK = 4
K_PASS = P * PACK
PASSES = K // K_PASS
M_TILES = N // P


def tile_picked_merge_lin_relu_sub_e_kernel(tc, xT, w, b, offs, out):
    nc = tc.nc
    x_rows = xT.rearrange("(a p j) t -> a p j t", a=PASSES, j=PACK)
    w_rows = w.rearrange("d (a p j) m -> d a p j m", a=PASSES, j=PACK)

    with ExitStack() as ctx:
        held = ctx.enter_context(tc.tile_pool(name="held", bufs=1))
        ring = ctx.enter_context(tc.tile_pool(name="ring", bufs=4))
        psum = ctx.enter_context(tc.psum_pool(name="psum", bufs=1))

        offsets = held.tile([P, S // 16], U16, name="offsets")
        bias_rows = held.tile([P, P], F32, name="bias_rows")
        bias = held.tile([P, M_TILES], F32, name="bias")
        ident = held.tile([P, P], F32, name="ident")
        planes, raws, groupeds, codes, scales = {}, {}, {}, {}, {}
        picked = [held.tile([P, PACK, S], F32, name=f"picked{a}") for a in range(PASSES)]
        x_codes = [held.tile([P, S], U32, align_bytes=64, name=f"x_codes{a}") for a in range(PASSES)]
        x_scales = [held.tile([P, S], U8, align_bytes=64, name=f"x_scales{a}") for a in range(PASSES)]
        acc = [psum.tile([P, V], F32, name=f"acc{t}") for t in range(M_TILES)]
        results = [held.tile([P, V], F32, name=f"result{t}") for t in range(M_TILES)]

        def load_x(a, j0):
            planes[a, j0] = held.tile([P, 2, T], F32, name=f"planes{a}{j0}")
            nc.sync.dma_start(planes[a, j0][:], x_rows[a, :, j0 : j0 + 2, :])

        def load_w(d, a, c0, c1):
            raws[d, a, c0] = held.tile([P, PACK, c1 - c0], F32, name=f"raw{d}{a}{c0}")
            nc.sync.dma_start(raws[d, a, c0][:], w_rows[d, a, :, :, c0:c1])

        def interleave(dst, src, c0, c1, engine_copy):
            engine_copy(
                dst[:, c0:c1, :].rearrange("p (c i) j -> p c j i", i=4),
                src[:, :, c0:c1].rearrange("p j (c i) -> p c j i", i=4),
            )

        def gather(a, j0):
            for u in range(2):
                nc.vector.tensor_copy(picked[a][:, j0 + u, :], planes[a, j0][:, u, :].indirect(offsets[:]))

        def spread_x(a, c0, c1):
            if c0 == 0:
                groupeds[a] = ring.tile([P, S, PACK], BF16, align_bytes=64, name="x_grouped")
            interleave(groupeds[a], picked[a], c0, c1, nc.scalar.copy)

        def quantise_x(a):
            nc.vector.quantize_mx(
                out=x_codes[a][:].bitcast(FP8X4),
                scales=x_scales[a][:],
                in_=groupeds[a][:].rearrange("p c j -> p (c j)"),
            )

        def spread_w(d, a, c0, c1, v_cols):
            width = c1 - c0
            grouped = ring.tile([P, width, PACK], BF16, align_bytes=64, name=f"w_grouped{width}")
            groupeds[d, a, c0] = grouped
            interleave(grouped, raws[d, a, c0], 0, v_cols, nc.vector.tensor_copy)
            interleave(grouped, raws[d, a, c0], v_cols, width, nc.scalar.copy)

        def quantise_w(d, a, c0, c1):
            codes[d, a, c0] = held.tile([P, c1 - c0], U32, align_bytes=64, name=f"w_codes{d}{a}{c0}")
            scales[d, a, c0] = held.tile([P, c1 - c0], U8, align_bytes=64, name=f"w_scales{d}{a}{c0}")
            nc.vector.quantize_mx(
                out=codes[d, a, c0][:].bitcast(FP8X4),
                scales=scales[d, a, c0][:],
                in_=groupeds[d, a, c0][:].rearrange("p c j -> p (c j)"),
            )

        def multiply(d, a, c0, c1, first=False, last=False):
            tokens = slice(d * V, (d + 1) * V)
            for m0 in range(c0, c1, P):
                cols = slice(m0 - c0, m0 - c0 + P)
                nc.tensor.matmul_mx(
                    out=acc[m0 // P][:],
                    lhsT=codes[d, a, c0][:, cols].bitcast(FP8X4),
                    lhsT_scale=scales[d, a, c0][:, cols],
                    rhs=x_codes[a][:, tokens].bitcast(FP8X4),
                    rhs_scale=x_scales[a][:, tokens],
                    start=first,
                    stop=last,
                )

        def finish(t, on_vector=False):
            if on_vector:
                nc.vector.tensor_scalar(results[t][:], acc[t][:], bias[:, t : t + 1], 0.0, op0=ADD, op1=MAX)
            else:
                nc.scalar.activation(results[t][:], acc[t][:], RELU, bias=bias[:, t : t + 1])
            nc.sync.dma_start(out[t * P : (t + 1) * P, :], results[t][:])

        nc.gpsimd.memset(bias_rows[:], 0.0)
        make_identity(nc, ident[:])
        turned = psum.tile([P, P], F32, name="turned")

        def turn_bias():
            nc.tensor.transpose(turned[:], bias_rows[:], ident[:])
            nc.vector.tensor_copy(bias[:], turned[:, 0:M_TILES])

        load_x(0, 0)
        nc.sync.dma_start(offsets[:], offs)
        load_x(0, 2)
        nc.sync.dma_start(bias_rows[0:M_TILES, :], b.rearrange("(t p) o -> t (p o)", p=P))
        load_x(1, 0)
        load_x(1, 2)
        chunks = [(d, a, 0, N) for a in range(PASSES) for d in range(D)][:-1]
        chunks += [(3, 1, 0, 256), (3, 1, 256, 384), (3, 1, 384, 512)]
        for chunk in chunks:
            load_w(*chunk)

        gather(0, 0)
        gather(0, 2)
        spread_x(0, 0, S)
        gather(1, 0)
        quantise_x(0)
        turn_bias()
        gather(1, 2)
        spread_w(*chunks[0], 224)
        spread_x(1, 0, 256)
        spread_w(*chunks[1], 224)
        quantise_w(*chunks[0])
        multiply(*chunks[0], first=True)
        spread_x(1, 256, S)
        spread_w(*chunks[2], 224)
        quantise_w(*chunks[1])
        multiply(*chunks[1])
        quantise_x(1)
        for before, now in zip(chunks[2:], chunks[3:]):
            spread_w(*now, 224 if now[3] - now[2] == N else (now[3] - now[2]) // 2)
            quantise_w(*before)
            multiply(*before, last=before[:2] == (3, 1))
        quantise_w(*chunks[-1])
        multiply(*chunks[-1], last=True)
        finish(0)
        finish(1)
        finish(2)
        finish(3, on_vector=True)
